import numpy as np
import ml_dtypes


def mxq(x, axis, fmt="e4m3"):
    dtype, down = {"e4m3": (ml_dtypes.float8_e4m3fn, 7), "e5m2": (ml_dtypes.float8_e5m2, 14)}[fmt]
    v = np.moveaxis(np.asarray(x, np.float32).astype(ml_dtypes.bfloat16).astype(np.float64), axis, -1)
    blocks = v.reshape(v.shape[:-1] + (-1, 32))
    amax = np.abs(blocks).max(-1, keepdims=True)
    byte = np.maximum(np.where(amax > 0, np.frexp(amax)[1] - 1 + 127, 0) - down, 1)
    scale = np.exp2(byte - 127.0)
    codes = (blocks / scale).astype(np.float32).astype(dtype).astype(np.float64)
    return np.moveaxis((codes * scale).reshape(v.shape), -1, axis)


WIDE = False


def mx_kscale(k):
    if not WIDE:
        return np.ones(k)
    levels = np.array([10, -10, 5, -5, 0])
    if k % 512:
        return np.exp2(np.random.permutation(np.resize(levels, k // 32))).repeat(32)
    a = np.empty((k // 512, 16))
    for p in range(k // 512):
        a[p, :8] = np.random.permutation(np.resize(levels, 8))
        for g in range(8):
            far = levels[np.abs(levels - a[p, g]) >= 10]
            a[p, g + 8] = far[np.random.randint(len(far))]
    return np.exp2(a.ravel()).repeat(32)


def f64(x):
    return np.asarray(x).astype(np.float64)


def striped8(idx):
    return np.asarray(idx).reshape(8, -1, 16).transpose(0, 2, 1).reshape(128, -1).astype(np.uint16)


def unstriped8(offs):
    return offs.reshape(8, 16, -1).transpose(0, 2, 1).reshape(8, -1).astype(np.int64)


def pick8(x, idx, run):
    r = np.arange(len(x))
    return x[r[:, None], idx[r % (8 * run) // run]]


E2M1 = np.array([0.0, 0.5, 1.0, 1.5, 2.0, 3.0, 4.0, 6.0, -0.0, -0.5, -1.0, -1.5, -2.0, -3.0, -4.0, -6.0])


def pack_weight(w, fmt):
    k, n = w.shape
    w = f64(np.asarray(w, np.float32).astype(ml_dtypes.bfloat16)).reshape(k // 32, 32, n)
    amax = np.abs(w).max(1)
    if fmt == "e4m3":
        byte = np.frexp(amax)[1] - 1 + 127 - 7
    else:
        mant, ex = np.frexp(amax / 6.0)
        byte = np.where(mant > 0.5, ex, ex - 1) + 127
    byte = np.clip(np.where(amax > 0, byte, 1), 1, 254)
    scaled = (w * np.exp2(127.0 - byte)[:, None, :]).reshape(k, n).astype(np.float32)
    by_word = np.ascontiguousarray(scaled.reshape(k // 512, 128, 4, n).transpose(0, 1, 3, 2))
    if fmt == "e4m3":
        words = by_word.astype(ml_dtypes.float8_e4m3fn).view(np.uint8)
    else:
        c = by_word.astype(ml_dtypes.float4_e2m1fn).view(np.uint8) & 0xF
        words = (c[..., 0::2] | (c[..., 1::2] << 4)).reshape(k // 512, 128, 2 * n)
    return np.ascontiguousarray(words), np.ascontiguousarray(byte.astype(np.uint8).reshape(k // 512, 16, n))


def unpack_weight(words, scales, fmt):
    g, _, n = scales.shape
    words = np.ascontiguousarray(words).reshape(g, 128, n, -1)
    if fmt == "e4m3":
        vals = words.view(ml_dtypes.float8_e4m3fn).astype(np.float64)
    else:
        nib = np.empty((g, 128, n, 4), np.uint8)
        nib[..., 0::2] = words & 0xF
        nib[..., 1::2] = words >> 4
        vals = E2M1[nib]
    vals = vals * np.repeat(np.exp2(scales.astype(np.float64) - 127.0), 8, axis=1)[..., None]
    return vals.transpose(0, 1, 3, 2).reshape(g * 512, n)


K, T, S, J, I = 512, 1024, 1024, 512, 512


def setup_inputs():
    n = np.random.standard_normal
    idx = np.stack([np.random.permutation(T)[:J] for _ in range(8)])
    idx2 = np.stack([np.random.permutation(S)[:I] for _ in range(8)])
    fk = mx_kscale(K)
    xap = pack_weight(n((K, T)) * 0.05 * fk[:, None], "e4m3")
    return {
        "xa_words": xap[0],
        "xa_scales": xap[1],
        "xb": (n((K, S)) / fk[:, None]).astype(np.float32),
        "cw1": (np.random.uniform(0.5, 2.0, (1, I))).astype(np.float32),
        "offs": striped8(idx),
        "offs2": striped8(idx2),
    }


def reference(xa_words, xa_scales, xb, cw1, offs, offs2):
    idx = unstriped8(offs)
    idx2 = unstriped8(offs2)
    xau = unpack_weight(xa_words, xa_scales, "e4m3")
    xaidxg = pick8(xau, idx, 64)
    xbidx2q = mxq(pick8(f64(xb), idx2, 64), 0, "e4m3")
    a = xaidxg.T @ xbidx2q
    y = np.tanh(a) * f64(cw1)
    return y

@@ -1,0 +1,138 @@
+from contextlib import ExitStack
+
+import concourse.mybir as mybir
+from concourse.masks import make_identity
+
+K, T, S, J, I = 512, 1024, 1024, 512, 512
+FLOPS = 2 * K * J * I
+
+F32 = mybir.dt.float32
+BF16 = mybir.dt.bfloat16
+I32 = mybir.dt.int32
+U32 = mybir.dt.uint32
+U16 = mybir.dt.uint16
+U8 = mybir.dt.uint8
+FP8X4 = mybir.dt.float8_e4m3fn_x4
+TANH = mybir.ActivationFunctionType.Tanh
+COPY = mybir.ActivationFunctionType.Copy
+MULT = mybir.AluOpType.mult
+
+P = 128
+PACK = 4
+HALF = I // 2
+QUARTER = I // 4
+
+
+def tile_moe_expert_choice_scores_by_group_kernel(tc, xa_words, xa_scales, xb, cw1, offs, offs2, out):
+    nc = tc.nc
+    with ExitStack() as ctx:
+        keep = ctx.enter_context(tc.tile_pool(name="keep", bufs=1))
+        psum = ctx.enter_context(tc.psum_pool(name="psum", bufs=1))
+
+        a_list = keep.tile([P, J // 16], U16)
+        b_list = keep.tile([P, I // 16], U16)
+        a_bytes = keep.tile([P, T], U8, align_bytes=64)
+        a_words = keep.tile([P, T], I32, align_bytes=64)
+        planes = [keep.tile([P, S], F32, name="plane%d" % t) for t in range(PACK)]
+        cw_cols = keep.tile([P, PACK], F32)
+        picked_bytes = keep.tile([P, J], U8, align_bytes=64)
+        a_scales = keep.tile([P, J], U8, align_bytes=64)
+        a_codes = keep.tile([P, J], U32, align_bytes=64)
+        picked = keep.tile([P, PACK, I], BF16, align_bytes=64)
+        ident = keep.tile([P, P], F32)
+        warm = keep.tile([P, 1], F32)
+
+        nc.vector.memset(a_scales[:].bitcast(I32), 0)
+        nc.scalar.dma_start(out=cw_cols[:], in_=cw1.rearrange("o (p c) -> (o p) c", c=PACK))
+
+        xb_rows = xb.rearrange("(p t) s -> p t s", t=PACK)
+        nc.sync.dma_start(a_list[:], offs)
+        nc.sync.dma_start(
+            out=a_bytes[:].bitcast(I32),
+            in_=xa_scales[0].bitcast(I32).unsqueeze(1).to_broadcast([16, 8, T // 4]),
+        )
+        nc.sync.dma_start(b_list[:], offs2)
+        nc.sync.dma_start(out=planes[0][:], in_=xb_rows[:, 0, :])
+        nc.sync.dma_start(out=planes[1][:], in_=xb_rows[:, 1, :])
+        nc.sync.dma_start(out=planes[2][:], in_=xb_rows[:, 2, :])
+        nc.sync.dma_start(out=planes[3][:], in_=xb_rows[:, 3, :])
+        nc.sync.dma_start(out=a_words[:], in_=xa_words[0].rearrange("p n t -> p (n t)").bitcast(I32))
+
+        make_identity(nc, ident[:])
+        nc.scalar.activation(out=warm[:], in_=ident[:, 0:1], func=TANH)
+
+        cw_bank = psum.tile([P, PACK, P], F32)
+        for c in range(PACK):
+            nc.tensor.transpose(cw_bank[:, c, :], cw_cols[:, c : c + 1].to_broadcast([P, P]), ident[:])
+
+        nc.vector.tensor_copy(picked_bytes[:], a_bytes[:].indirect(a_list[:]))
+        for x in range(4):
+            nc.scalar.dma_start(
+                out=a_scales[32 * x : 32 * x + 4, :].bitcast(I32),
+                in_=picked_bytes[32 * x : 32 * x + 32 : 8, :].bitcast(I32),
+            )
+
+        plane0_bf16 = keep.tile([P, S], BF16)
+        nc.scalar.activation(out=plane0_bf16[:], in_=planes[0][:], func=COPY)
+        nc.scalar.activation(out=picked[:, 0, :], in_=plane0_bf16[:].indirect(b_list[:]), func=COPY)
+        nc.vector.tensor_copy(picked[:, 1, :], planes[1][:].indirect(b_list[:]))
+        nc.vector.tensor_copy(picked[:, 2, :], planes[2][:].indirect(b_list[:]))
+        for h in range(2):
+            nc.vector.tensor_copy(
+                picked[:, 3, h * HALF : (h + 1) * HALF],
+                planes[3][:].indirect(b_list[:, h * HALF // 16 : (h + 1) * HALF // 16]),
+            )
+
+        def weave(engine_copy, woven, h, first, count):
+            src = picked[:, :, h * HALF + first : h * HALF + first + count].rearrange("p t (c e) -> p c t e", e=4)
+            dst = woven[:, first : first + count, :].rearrange("p (c e) t -> p c t e", e=4)
+            engine_copy(out=dst, in_=src)
+
+        b_codes = []
+        b_scales = []
+        for h in range(2):
+            woven = keep.tile([P, HALF, PACK], BF16, align_bytes=64, name="woven%d" % h)
+            if h == 0:
+                weave(nc.scalar.copy, woven, h, 0, QUARTER)
+                weave(nc.vector.tensor_copy, woven, h, QUARTER, QUARTER)
+            else:
+                weave(nc.scalar.copy, woven, h, 0, HALF)
+            codes = keep.tile([P, HALF], U32, align_bytes=64, name="b_codes%d" % h)
+            scales = keep.tile([P, HALF], U8, align_bytes=64, name="b_scales%d" % h)
+            nc.vector.quantize_mx(out=codes[:].bitcast(FP8X4), scales=scales[:], in_=woven[:].rearrange("p n t -> p (n t)"))
+            b_codes.append(codes)
+            b_scales.append(scales)
+            if h == 0:
+                for g in range(2):
+                    nc.vector.tensor_copy(
+                        a_codes[:, g * J // 2 : (g + 1) * J // 2],
+                        a_words[:].bitcast(U32).indirect(a_list[:, g * J // 32 : (g + 1) * J // 32]),
+                    )
+
+        out_rows = out.rearrange("(r p) i -> p r i", p=P)
+        for h in range(2):
+            cw = cw_bank[:, :, h * HALF // PACK : (h + 1) * HALF // PACK].rearrange("m c p -> m p c")
+            cw = cw.unsqueeze(1).to_broadcast([P, 2, HALF // PACK, PACK])
+            for g in range(2):
+                acc = psum.tile([P, 2, HALF], F32, name="acc%d%d" % (h, g))
+                for r in range(2):
+                    rows = slice((2 * g + r) * P, (2 * g + r + 1) * P)
+                    nc.tensor.matmul_mx(
+                        out=acc[:, r, :],
+                        lhsT=a_codes[:, rows].bitcast(FP8X4),
+                        lhsT_scale=a_scales[:, rows],
+                        rhs=b_codes[h][:].bitcast(FP8X4),
+                        rhs_scale=b_scales[h][:],
+                        start=True,
+                        stop=True,
+                    )
+                squashed = keep.tile([P, 2, HALF], F32, name="squashed%d%d" % (h, g))
+                nc.scalar.activation(out=squashed[:], in_=acc[:], func=TANH)
+                result = keep.tile([P, 2, HALF], F32, name="result%d%d" % (h, g))
+                nc.vector.tensor_tensor(
+                    out=result[:].rearrange("p r (n c) -> p r n c", c=PACK),
+                    in0=squashed[:].rearrange("p r (n c) -> p r n c", c=PACK),
+                    in1=cw,
+                    op=MULT,
+                )
+                nc.sync.dma_start(out=out_rows[:, 2 * g : 2 * g + 2, h * HALF : (h + 1) * HALF], in_=result[:])

@@ -20,7 +20,8 @@ MULT = mybir.AluOpType.mult
 P = 128
 PACK = 4
 HALF = I // 2
-QUARTER = I // 4
+SCALAR_SHARE = 192
+GPSIMD_PIECES = 2
 
 
 def tile_moe_expert_choice_scores_by_group_kernel(tc, xa_words, xa_scales, xb, cw1, offs, offs2, out):
@@ -32,107 +33,123 @@ def tile_moe_expert_choice_scores_by_group_kernel(tc, xa_words, xa_scales, xb, c
         a_list = keep.tile([P, J // 16], U16)
         b_list = keep.tile([P, I // 16], U16)
         a_bytes = keep.tile([P, T], U8, align_bytes=64)
-        a_words = keep.tile([P, T], I32, align_bytes=64)
-        planes = [keep.tile([P, S], F32, name="plane%d" % t) for t in range(PACK)]
+        a_words = keep.tile([P, T], I32, align_bytes=64, tag="a_words")
+        plane0 = [keep.tile([P, S // 2], F32, name="plane0_%d" % u) for u in range(2)]
+        planes = {t: keep.tile([P, S], F32, name="plane%d" % t) for t in range(1, PACK)}
         cw_cols = keep.tile([P, PACK], F32)
         picked_bytes = keep.tile([P, J], U8, align_bytes=64)
         a_scales = keep.tile([P, J], U8, align_bytes=64)
-        a_codes = keep.tile([P, J], U32, align_bytes=64)
-        picked = keep.tile([P, PACK, I], BF16, align_bytes=64)
+        picked = [keep.tile([P, PACK, HALF], BF16, align_bytes=64, name="picked%d" % h) for h in range(2)]
         ident = keep.tile([P, P], F32)
         warm = keep.tile([P, 1], F32)
 
+        nc.gpsimd.memset(a_bytes[:].bitcast(I32), 0)
+        zero = keep.tile([P, 1], F32)
+        nc.vector.memset(zero[:], 0.0)
         nc.vector.memset(a_scales[:].bitcast(I32), 0)
         nc.scalar.dma_start(out=cw_cols[:], in_=cw1.rearrange("o (p c) -> (o p) c", c=PACK))
 
         xb_rows = xb.rearrange("(p t) s -> p t s", t=PACK)
         nc.sync.dma_start(a_list[:], offs)
-        nc.sync.dma_start(
-            out=a_bytes[:].bitcast(I32),
-            in_=xa_scales[0].bitcast(I32).unsqueeze(1).to_broadcast([16, 8, T // 4]),
-        )
         nc.sync.dma_start(b_list[:], offs2)
-        nc.sync.dma_start(out=planes[0][:], in_=xb_rows[:, 0, :])
+        for u in range(2):
+            nc.sync.dma_start(out=plane0[u][:], in_=xb_rows[:, 0, u * S // 2 : (u + 1) * S // 2])
+        nc.sync.dma_start(out=a_bytes[0:P:8, :].bitcast(I32), in_=xa_scales[0].bitcast(I32))
         nc.sync.dma_start(out=planes[1][:], in_=xb_rows[:, 1, :])
         nc.sync.dma_start(out=planes[2][:], in_=xb_rows[:, 2, :])
         nc.sync.dma_start(out=planes[3][:], in_=xb_rows[:, 3, :])
         nc.sync.dma_start(out=a_words[:], in_=xa_words[0].rearrange("p n t -> p (n t)").bitcast(I32))
 
         make_identity(nc, ident[:])
-        nc.scalar.activation(out=warm[:], in_=ident[:, 0:1], func=TANH)
+        nc.scalar.activation(out=warm[:], in_=zero[:], func=TANH)
+
 
         cw_bank = psum.tile([P, PACK, P], F32)
         for c in range(PACK):
             nc.tensor.transpose(cw_bank[:, c, :], cw_cols[:, c : c + 1].to_broadcast([P, P]), ident[:])
 
+        cw_rows = keep.tile([P, HALF], F32)
+        nc.vector.tensor_copy(
+            out=cw_rows[:].rearrange("m (p c) -> m p c", c=PACK),
+            in_=cw_bank[:, :, 0 : HALF // PACK].rearrange("m c p -> m p c"),
+        )
+
         nc.vector.tensor_copy(picked_bytes[:], a_bytes[:].indirect(a_list[:]))
         for x in range(4):
-            nc.scalar.dma_start(
+            nc.sync.dma_start(
                 out=a_scales[32 * x : 32 * x + 4, :].bitcast(I32),
                 in_=picked_bytes[32 * x : 32 * x + 32 : 8, :].bitcast(I32),
             )
 
-        plane0_bf16 = keep.tile([P, S], BF16)
-        nc.scalar.activation(out=plane0_bf16[:], in_=planes[0][:], func=COPY)
-        nc.scalar.activation(out=picked[:, 0, :], in_=plane0_bf16[:].indirect(b_list[:]), func=COPY)
-        nc.vector.tensor_copy(picked[:, 1, :], planes[1][:].indirect(b_list[:]))
-        nc.vector.tensor_copy(picked[:, 2, :], planes[2][:].indirect(b_list[:]))
+        b_lists = [b_list[:, h * HALF // 16 : (h + 1) * HALF // 16] for h in range(2)]
+        rounded0 = keep.tile([P, S], BF16)
+        for u in range(2):
+            nc.scalar.activation(out=rounded0[:, u * S // 2 : (u + 1) * S // 2], in_=plane0[u][:], func=COPY)
         for h in range(2):
-            nc.vector.tensor_copy(
-                picked[:, 3, h * HALF : (h + 1) * HALF],
-                planes[3][:].indirect(b_list[:, h * HALF // 16 : (h + 1) * HALF // 16]),
+            nc.scalar.activation(out=picked[h][:, 0, :], in_=rounded0[:].indirect(b_lists[h]), func=COPY)
+        rounded2 = keep.tile([P, S], BF16)
+        nc.scalar.activation(out=rounded2[:], in_=planes[2][:], func=COPY)
+        nc.scalar.activation(out=picked[1][:, 2, :], in_=rounded2[:].indirect(b_lists[1]), func=COPY)
+        for t, halves in ((1, (0, 1)), (2, (0,)), (3, (0, 1))):
+            for h in halves:
+                nc.vector.tensor_copy(picked[h][:, t, :], planes[t][:].indirect(b_lists[h]))
+
+        woven = [keep.tile([P, HALF, PACK], BF16, align_bytes=64, name="woven%d" % h, tag="woven%d" % h) for h in range(2)]
+
+        def weave(engine_copy, h, cols):
+            engine_copy(
+                out=woven[h][:, cols, :].rearrange("p (c e) t -> p c t e", e=4),
+                in_=picked[h][:, :, cols].rearrange("p t (c e) -> p c t e", e=4),
             )
 
-        def weave(engine_copy, woven, h, first, count):
-            src = picked[:, :, h * HALF + first : h * HALF + first + count].rearrange("p t (c e) -> p c t e", e=4)
-            dst = woven[:, first : first + count, :].rearrange("p (c e) t -> p c t e", e=4)
-            engine_copy(out=dst, in_=src)
+        def gather_words(first, count, tag):
+            words = keep.tile([P, count * P], U32, align_bytes=64, name="a_codes%d" % first, tag=tag)
+            blocks = [words[:, n * P : (n + 1) * P] for n in range(count)]
+            for n in range(count):
+                entries = a_list[:, (first + n) * P // 16 : (first + n + 1) * P // 16]
+                nc.vector.tensor_copy(blocks[n], a_words[:].bitcast(U32).indirect(entries))
+            return blocks
 
-        b_codes = []
-        b_scales = []
-        for h in range(2):
-            woven = keep.tile([P, HALF, PACK], BF16, align_bytes=64, name="woven%d" % h)
-            if h == 0:
-                weave(nc.scalar.copy, woven, h, 0, QUARTER)
-                weave(nc.vector.tensor_copy, woven, h, QUARTER, QUARTER)
-            else:
-                weave(nc.scalar.copy, woven, h, 0, HALF)
+        def quantise(h):
             codes = keep.tile([P, HALF], U32, align_bytes=64, name="b_codes%d" % h)
             scales = keep.tile([P, HALF], U8, align_bytes=64, name="b_scales%d" % h)
-            nc.vector.quantize_mx(out=codes[:].bitcast(FP8X4), scales=scales[:], in_=woven[:].rearrange("p n t -> p (n t)"))
-            b_codes.append(codes)
-            b_scales.append(scales)
-            if h == 0:
-                for g in range(2):
-                    nc.vector.tensor_copy(
-                        a_codes[:, g * J // 2 : (g + 1) * J // 2],
-                        a_words[:].bitcast(U32).indirect(a_list[:, g * J // 32 : (g + 1) * J // 32]),
-                    )
+            nc.vector.quantize_mx(out=codes[:].bitcast(FP8X4), scales=scales[:], in_=woven[h][:].rearrange("p n t -> p (n t)"))
+            return codes, scales
 
-        out_rows = out.rearrange("(r p) i -> p r i", p=P)
-        for h in range(2):
-            cw = cw_bank[:, :, h * HALF // PACK : (h + 1) * HALF // PACK].rearrange("m c p -> m p c")
-            cw = cw.unsqueeze(1).to_broadcast([P, 2, HALF // PACK, PACK])
-            for g in range(2):
-                acc = psum.tile([P, 2, HALF], F32, name="acc%d%d" % (h, g))
-                for r in range(2):
-                    rows = slice((2 * g + r) * P, (2 * g + r + 1) * P)
-                    nc.tensor.matmul_mx(
-                        out=acc[:, r, :],
-                        lhsT=a_codes[:, rows].bitcast(FP8X4),
-                        lhsT_scale=a_scales[:, rows],
-                        rhs=b_codes[h][:].bitcast(FP8X4),
-                        rhs_scale=b_scales[h][:],
-                        start=True,
-                        stop=True,
-                    )
-                squashed = keep.tile([P, 2, HALF], F32, name="squashed%d%d" % (h, g))
-                nc.scalar.activation(out=squashed[:], in_=acc[:], func=TANH)
-                result = keep.tile([P, 2, HALF], F32, name="result%d%d" % (h, g))
+        weave(nc.scalar.copy, 0, slice(0, SCALAR_SHARE))
+        weave(nc.vector.tensor_copy, 0, slice(SCALAR_SHARE, HALF))
+        weave(nc.scalar.copy, 1, slice(0, HALF))
+        a_codes = gather_words(0, 1, "a_codes0")
+        b_quantised = [quantise(0)]
+        a_codes = a_codes + gather_words(1, 2, "woven0")
+        b_quantised.append(quantise(1))
+        a_codes = a_codes + gather_words(3, 1, "woven1")
+
+        out_blocks = out.rearrange("(r p) (h n) -> p r h n", p=P, n=HALF)
+        cw_halves = cw_bank[:].rearrange("m c (h p) -> m h p c", h=2)
+        pieces = [(r, h) for h in range(2) for r in range(3)] + [(3, h) for h in range(2)]
+        for number, (r, h) in enumerate(pieces):
+            b_codes, b_scales = b_quantised[h]
+            acc = psum.tile([P, HALF], F32, name="acc", bufs=7)
+            nc.tensor.matmul_mx(
+                out=acc[:],
+                lhsT=a_codes[r].bitcast(FP8X4),
+                lhsT_scale=a_scales[:, r * P : (r + 1) * P],
+                rhs=b_codes[:].bitcast(FP8X4),
+                rhs_scale=b_scales[:],
+                start=True,
+                stop=True,
+            )
+            squashed = keep.tile([P, HALF], F32, name="squashed%d" % number)
+            nc.scalar.activation(out=squashed[:], in_=acc[:], func=TANH)
+            result = keep.tile([P, HALF], F32, name="result%d" % number)
+            if number < GPSIMD_PIECES:
+                nc.gpsimd.tensor_tensor(out=result[:], in0=squashed[:], in1=cw_rows[:], op=MULT)
+            else:
                 nc.vector.tensor_tensor(
-                    out=result[:].rearrange("p r (n c) -> p r n c", c=PACK),
-                    in0=squashed[:].rearrange("p r (n c) -> p r n c", c=PACK),
-                    in1=cw,
+                    out=result[:].rearrange("p (n c) -> p n c", c=PACK),
+                    in0=squashed[:].rearrange("p (n c) -> p n c", c=PACK),
+                    in1=cw_halves[:, h],
                     op=MULT,
                 )
-                nc.sync.dma_start(out=out_rows[:, 2 * g : 2 * g + 2, h * HALF : (h + 1) * HALF], in_=result[:])
+            nc.sync.dma_start(out=out_blocks[:, r, h, :], in_=result[:])

@@ -19,9 +19,14 @@ MULT = mybir.AluOpType.mult
 
 P = 128
 PACK = 4
+GROUP = 16
+BLOCK_ROWS = 8
+QUADRANT = 32
 HALF = I // 2
+RUN = 4
 SCALAR_SHARE = 192
-GPSIMD_PIECES = 2
+GPSIMD_PIECES = (0, 2)
+ACC_BANKS = 7
 
 
 def tile_moe_expert_choice_scores_by_group_kernel(tc, xa_words, xa_scales, xb, cw1, offs, offs2, out):
@@ -30,10 +35,10 @@ def tile_moe_expert_choice_scores_by_group_kernel(tc, xa_words, xa_scales, xb, c
         keep = ctx.enter_context(tc.tile_pool(name="keep", bufs=1))
         psum = ctx.enter_context(tc.psum_pool(name="psum", bufs=1))
 
-        a_list = keep.tile([P, J // 16], U16)
-        b_list = keep.tile([P, I // 16], U16)
+        a_list = keep.tile([P, J // GROUP], U16)
+        b_list = keep.tile([P, I // GROUP], U16)
         a_bytes = keep.tile([P, T], U8, align_bytes=64)
-        a_words = keep.tile([P, T], I32, align_bytes=64, tag="a_words")
+        a_words = keep.tile([P, T], I32, align_bytes=64)
         plane0 = [keep.tile([P, S // 2], F32, name="plane0_%d" % u) for u in range(2)]
         planes = {t: keep.tile([P, S], F32, name="plane%d" % t) for t in range(1, PACK)}
         cw_cols = keep.tile([P, PACK], F32)
@@ -47,41 +52,37 @@ def tile_moe_expert_choice_scores_by_group_kernel(tc, xa_words, xa_scales, xb, c
         zero = keep.tile([P, 1], F32)
         nc.vector.memset(zero[:], 0.0)
         nc.vector.memset(a_scales[:].bitcast(I32), 0)
-        nc.scalar.dma_start(out=cw_cols[:], in_=cw1.rearrange("o (p c) -> (o p) c", c=PACK))
 
+        nc.scalar.dma_start(out=cw_cols[:], in_=cw1.rearrange("o (p c) -> (o p) c", c=PACK))
         xb_rows = xb.rearrange("(p t) s -> p t s", t=PACK)
-        nc.sync.dma_start(a_list[:], offs)
-        nc.sync.dma_start(b_list[:], offs2)
         for u in range(2):
             nc.sync.dma_start(out=plane0[u][:], in_=xb_rows[:, 0, u * S // 2 : (u + 1) * S // 2])
-        nc.sync.dma_start(out=a_bytes[0:P:8, :].bitcast(I32), in_=xa_scales[0].bitcast(I32))
-        nc.sync.dma_start(out=planes[1][:], in_=xb_rows[:, 1, :])
-        nc.sync.dma_start(out=planes[2][:], in_=xb_rows[:, 2, :])
-        nc.sync.dma_start(out=planes[3][:], in_=xb_rows[:, 3, :])
+        nc.sync.dma_start(b_list[:], offs2)
+        nc.sync.dma_start(a_list[:], offs)
+        nc.sync.dma_start(out=a_bytes[0:P:BLOCK_ROWS, :].bitcast(I32), in_=xa_scales[0].bitcast(I32))
+        for t in range(1, PACK):
+            nc.sync.dma_start(out=planes[t][:], in_=xb_rows[:, t, :])
         nc.sync.dma_start(out=a_words[:], in_=xa_words[0].rearrange("p n t -> p (n t)").bitcast(I32))
 
         make_identity(nc, ident[:])
         nc.scalar.activation(out=warm[:], in_=zero[:], func=TANH)
 
-
         cw_bank = psum.tile([P, PACK, P], F32)
         for c in range(PACK):
             nc.tensor.transpose(cw_bank[:, c, :], cw_cols[:, c : c + 1].to_broadcast([P, P]), ident[:])
-
-        cw_rows = keep.tile([P, HALF], F32)
-        nc.vector.tensor_copy(
-            out=cw_rows[:].rearrange("m (p c) -> m p c", c=PACK),
-            in_=cw_bank[:, :, 0 : HALF // PACK].rearrange("m c p -> m p c"),
-        )
+        cw_halves = cw_bank[:].rearrange("m c (h p) -> m h p c", h=2)
+        cw_half0 = keep.tile([P, HALF], F32)
+        nc.vector.tensor_copy(out=cw_half0[:].rearrange("m (p c) -> m p c", c=PACK), in_=cw_halves[:, 0])
 
         nc.vector.tensor_copy(picked_bytes[:], a_bytes[:].indirect(a_list[:]))
-        for x in range(4):
+        for x in range(P // QUADRANT):
+            first = QUADRANT * x
             nc.sync.dma_start(
-                out=a_scales[32 * x : 32 * x + 4, :].bitcast(I32),
-                in_=picked_bytes[32 * x : 32 * x + 32 : 8, :].bitcast(I32),
+                out=a_scales[first : first + QUADRANT // BLOCK_ROWS, :].bitcast(I32),
+                in_=picked_bytes[first : first + QUADRANT : BLOCK_ROWS, :].bitcast(I32),
             )
 
-        b_lists = [b_list[:, h * HALF // 16 : (h + 1) * HALF // 16] for h in range(2)]
+        b_lists = [b_list[:, h * HALF // GROUP : (h + 1) * HALF // GROUP] for h in range(2)]
         rounded0 = keep.tile([P, S], BF16)
         for u in range(2):
             nc.scalar.activation(out=rounded0[:, u * S // 2 : (u + 1) * S // 2], in_=plane0[u][:], func=COPY)
@@ -98,15 +99,15 @@ def tile_moe_expert_choice_scores_by_group_kernel(tc, xa_words, xa_scales, xb, c
 
         def weave(engine_copy, h, cols):
             engine_copy(
-                out=woven[h][:, cols, :].rearrange("p (c e) t -> p c t e", e=4),
-                in_=picked[h][:, :, cols].rearrange("p t (c e) -> p c t e", e=4),
+                out=woven[h][:, cols, :].rearrange("p (c e) t -> p c t e", e=RUN),
+                in_=picked[h][:, :, cols].rearrange("p t (c e) -> p c t e", e=RUN),
             )
 
         def gather_words(first, count, tag):
             words = keep.tile([P, count * P], U32, align_bytes=64, name="a_codes%d" % first, tag=tag)
             blocks = [words[:, n * P : (n + 1) * P] for n in range(count)]
             for n in range(count):
-                entries = a_list[:, (first + n) * P // 16 : (first + n + 1) * P // 16]
+                entries = a_list[:, (first + n) * P // GROUP : (first + n + 1) * P // GROUP]
                 nc.vector.tensor_copy(blocks[n], a_words[:].bitcast(U32).indirect(entries))
             return blocks
 
@@ -126,11 +127,11 @@ def tile_moe_expert_choice_scores_by_group_kernel(tc, xa_words, xa_scales, xb, c
         a_codes = a_codes + gather_words(3, 1, "woven1")
 
         out_blocks = out.rearrange("(r p) (h n) -> p r h n", p=P, n=HALF)
-        cw_halves = cw_bank[:].rearrange("m c (h p) -> m h p c", h=2)
-        pieces = [(r, h) for h in range(2) for r in range(3)] + [(3, h) for h in range(2)]
+        last_block = J // P - 1
+        pieces = [(r, h) for h in range(2) for r in range(last_block)] + [(last_block, h) for h in range(2)]
         for number, (r, h) in enumerate(pieces):
             b_codes, b_scales = b_quantised[h]
-            acc = psum.tile([P, HALF], F32, name="acc", bufs=7)
+            acc = psum.tile([P, HALF], F32, name="acc", bufs=ACC_BANKS)
             nc.tensor.matmul_mx(
                 out=acc[:],
                 lhsT=a_codes[r].bitcast(FP8X4),
@@ -143,8 +144,8 @@ def tile_moe_expert_choice_scores_by_group_kernel(tc, xa_words, xa_scales, xb, c
             squashed = keep.tile([P, HALF], F32, name="squashed%d" % number)
             nc.scalar.activation(out=squashed[:], in_=acc[:], func=TANH)
             result = keep.tile([P, HALF], F32, name="result%d" % number)
-            if number < GPSIMD_PIECES:
-                nc.gpsimd.tensor_tensor(out=result[:], in0=squashed[:], in1=cw_rows[:], op=MULT)
+            if number in GPSIMD_PIECES:
+                nc.gpsimd.tensor_tensor(out=result[:], in0=squashed[:], in1=cw_half0[:], op=MULT)
             else:
                 nc.vector.tensor_tensor(
                     out=result[:].rearrange("p (n c) -> p n c", c=PACK),

from contextlib import ExitStack

import concourse.mybir as mybir
from concourse.masks import make_identity

K, T, S, J, I = 512, 1024, 1024, 512, 512
FLOPS = 2 * K * J * I

F32 = mybir.dt.float32
BF16 = mybir.dt.bfloat16
I32 = mybir.dt.int32
U32 = mybir.dt.uint32
U16 = mybir.dt.uint16
U8 = mybir.dt.uint8
FP8X4 = mybir.dt.float8_e4m3fn_x4
TANH = mybir.ActivationFunctionType.Tanh
COPY = mybir.ActivationFunctionType.Copy
MULT = mybir.AluOpType.mult

P = 128
PACK = 4
GROUP = 16
BLOCK_ROWS = 8
QUADRANT = 32
HALF = I // 2
RUN = 4
SCALAR_SHARE = 192
GPSIMD_PIECES = (0, 2)
ACC_BANKS = 7


def tile_moe_expert_choice_scores_by_group_kernel(tc, xa_words, xa_scales, xb, cw1, offs, offs2, out):
    nc = tc.nc
    with ExitStack() as ctx:
        keep = ctx.enter_context(tc.tile_pool(name="keep", bufs=1))
        psum = ctx.enter_context(tc.psum_pool(name="psum", bufs=1))

        a_list = keep.tile([P, J // GROUP], U16)
        b_list = keep.tile([P, I // GROUP], U16)
        a_bytes = keep.tile([P, T], U8, align_bytes=64)
        a_words = keep.tile([P, T], I32, align_bytes=64)
        plane0 = [keep.tile([P, S // 2], F32, name="plane0_%d" % u) for u in range(2)]
        planes = {t: keep.tile([P, S], F32, name="plane%d" % t) for t in range(1, PACK)}
        cw_cols = keep.tile([P, PACK], F32)
        picked_bytes = keep.tile([P, J], U8, align_bytes=64)
        a_scales = keep.tile([P, J], U8, align_bytes=64)
        picked = [keep.tile([P, PACK, HALF], BF16, align_bytes=64, name="picked%d" % h) for h in range(2)]
        ident = keep.tile([P, P], F32)
        warm = keep.tile([P, 1], F32)

        nc.gpsimd.memset(a_bytes[:].bitcast(I32), 0)
        zero = keep.tile([P, 1], F32)
        nc.vector.memset(zero[:], 0.0)
        nc.vector.memset(a_scales[:].bitcast(I32), 0)

        nc.scalar.dma_start(out=cw_cols[:], in_=cw1.rearrange("o (p c) -> (o p) c", c=PACK))
        xb_rows = xb.rearrange("(p t) s -> p t s", t=PACK)
        for u in range(2):
            nc.sync.dma_start(out=plane0[u][:], in_=xb_rows[:, 0, u * S // 2 : (u + 1) * S // 2])
        nc.sync.dma_start(b_list[:], offs2)
        nc.sync.dma_start(a_list[:], offs)
        nc.sync.dma_start(out=a_bytes[0:P:BLOCK_ROWS, :].bitcast(I32), in_=xa_scales[0].bitcast(I32))
        for t in range(1, PACK):
            nc.sync.dma_start(out=planes[t][:], in_=xb_rows[:, t, :])
        nc.sync.dma_start(out=a_words[:], in_=xa_words[0].rearrange("p n t -> p (n t)").bitcast(I32))

        make_identity(nc, ident[:])
        nc.scalar.activation(out=warm[:], in_=zero[:], func=TANH)

        cw_bank = psum.tile([P, PACK, P], F32)
        for c in range(PACK):
            nc.tensor.transpose(cw_bank[:, c, :], cw_cols[:, c : c + 1].to_broadcast([P, P]), ident[:])
        cw_halves = cw_bank[:].rearrange("m c (h p) -> m h p c", h=2)
        cw_half0 = keep.tile([P, HALF], F32)
        nc.vector.tensor_copy(out=cw_half0[:].rearrange("m (p c) -> m p c", c=PACK), in_=cw_halves[:, 0])

        nc.vector.tensor_copy(picked_bytes[:], a_bytes[:].indirect(a_list[:]))
        for x in range(P // QUADRANT):
            first = QUADRANT * x
            nc.sync.dma_start(
                out=a_scales[first : first + QUADRANT // BLOCK_ROWS, :].bitcast(I32),
                in_=picked_bytes[first : first + QUADRANT : BLOCK_ROWS, :].bitcast(I32),
            )

        b_lists = [b_list[:, h * HALF // GROUP : (h + 1) * HALF // GROUP] for h in range(2)]
        rounded0 = keep.tile([P, S], BF16)
        for u in range(2):
            nc.scalar.activation(out=rounded0[:, u * S // 2 : (u + 1) * S // 2], in_=plane0[u][:], func=COPY)
        for h in range(2):
            nc.scalar.activation(out=picked[h][:, 0, :], in_=rounded0[:].indirect(b_lists[h]), func=COPY)
        rounded2 = keep.tile([P, S], BF16)
        nc.scalar.activation(out=rounded2[:], in_=planes[2][:], func=COPY)
        nc.scalar.activation(out=picked[1][:, 2, :], in_=rounded2[:].indirect(b_lists[1]), func=COPY)
        for t, halves in ((1, (0, 1)), (2, (0,)), (3, (0, 1))):
            for h in halves:
                nc.vector.tensor_copy(picked[h][:, t, :], planes[t][:].indirect(b_lists[h]))

        woven = [keep.tile([P, HALF, PACK], BF16, align_bytes=64, name="woven%d" % h, tag="woven%d" % h) for h in range(2)]

        def weave(engine_copy, h, cols):
            engine_copy(
                out=woven[h][:, cols, :].rearrange("p (c e) t -> p c t e", e=RUN),
                in_=picked[h][:, :, cols].rearrange("p t (c e) -> p c t e", e=RUN),
            )

        def gather_words(first, count, tag):
            words = keep.tile([P, count * P], U32, align_bytes=64, name="a_codes%d" % first, tag=tag)
            blocks = [words[:, n * P : (n + 1) * P] for n in range(count)]
            for n in range(count):
                entries = a_list[:, (first + n) * P // GROUP : (first + n + 1) * P // GROUP]
                nc.vector.tensor_copy(blocks[n], a_words[:].bitcast(U32).indirect(entries))
            return blocks

        def quantise(h):
            codes = keep.tile([P, HALF], U32, align_bytes=64, name="b_codes%d" % h)
            scales = keep.tile([P, HALF], U8, align_bytes=64, name="b_scales%d" % h)
            nc.vector.quantize_mx(out=codes[:].bitcast(FP8X4), scales=scales[:], in_=woven[h][:].rearrange("p n t -> p (n t)"))
            return codes, scales

        weave(nc.scalar.copy, 0, slice(0, SCALAR_SHARE))
        weave(nc.vector.tensor_copy, 0, slice(SCALAR_SHARE, HALF))
        weave(nc.scalar.copy, 1, slice(0, HALF))
        a_codes = gather_words(0, 1, "a_codes0")
        b_quantised = [quantise(0)]
        a_codes = a_codes + gather_words(1, 2, "woven0")
        b_quantised.append(quantise(1))
        a_codes = a_codes + gather_words(3, 1, "woven1")

        out_blocks = out.rearrange("(r p) (h n) -> p r h n", p=P, n=HALF)
        last_block = J // P - 1
        pieces = [(r, h) for h in range(2) for r in range(last_block)] + [(last_block, h) for h in range(2)]
        for number, (r, h) in enumerate(pieces):
            b_codes, b_scales = b_quantised[h]
            acc = psum.tile([P, HALF], F32, name="acc", bufs=ACC_BANKS)
            nc.tensor.matmul_mx(
                out=acc[:],
                lhsT=a_codes[r].bitcast(FP8X4),
                lhsT_scale=a_scales[:, r * P : (r + 1) * P],
                rhs=b_codes[:].bitcast(FP8X4),
                rhs_scale=b_scales[:],
                start=True,
                stop=True,
            )
            squashed = keep.tile([P, HALF], F32, name="squashed%d" % number)
            nc.scalar.activation(out=squashed[:], in_=acc[:], func=TANH)
            result = keep.tile([P, HALF], F32, name="result%d" % number)
            if number in GPSIMD_PIECES:
                nc.gpsimd.tensor_tensor(out=result[:], in0=squashed[:], in1=cw_half0[:], op=MULT)
            else:
                nc.vector.tensor_tensor(
                    out=result[:].rearrange("p (n c) -> p n c", c=PACK),
                    in0=squashed[:].rearrange("p (n c) -> p n c", c=PACK),
                    in1=cw_halves[:, h],
                    op=MULT,
                )
            nc.sync.dma_start(out=out_blocks[:, r, h, :], in_=result[:])
